import numpy as np
import ml_dtypes


def mxq(x, axis, fmt="e4m3"):
    dtype, down = {"e4m3": (ml_dtypes.float8_e4m3fn, 7), "e5m2": (ml_dtypes.float8_e5m2, 14)}[fmt]
    v = np.moveaxis(np.asarray(x, np.float32).astype(ml_dtypes.bfloat16).astype(np.float64), axis, -1)
    blocks = v.reshape(v.shape[:-1] + (-1, 32))
    amax = np.abs(blocks).max(-1, keepdims=True)
    byte = np.maximum(np.where(amax > 0, np.frexp(amax)[1] - 1 + 127, 0) - down, 1)
    scale = np.exp2(byte - 127.0)
    codes = (blocks / scale).astype(np.float32).astype(dtype).astype(np.float64)
    return np.moveaxis((codes * scale).reshape(v.shape), -1, axis)


WIDE = False


def mx_kscale(k):
    if not WIDE:
        return np.ones(k)
    levels = np.array([10, -10, 5, -5, 0])
    if k % 512:
        return np.exp2(np.random.permutation(np.resize(levels, k // 32))).repeat(32)
    a = np.empty((k // 512, 16))
    for p in range(k // 512):
        a[p, :8] = np.random.permutation(np.resize(levels, 8))
        for g in range(8):
            far = levels[np.abs(levels - a[p, g]) >= 10]
            a[p, g + 8] = far[np.random.randint(len(far))]
    return np.exp2(a.ravel()).repeat(32)


def f64(x):
    return np.asarray(x).astype(np.float64)


def striped(idx):
    return np.tile(idx.reshape(-1, 16).T, (8, 1)).astype(np.uint16)


def unstriped(offs):
    return offs[:16].T.reshape(-1).astype(np.int64)


def relu(v):
    return np.maximum(v, 0.0)


K, T, S, N = 2048, 1024, 512, 512


def setup_inputs():
    n = np.random.standard_normal
    s = mx_kscale(K)[:, None]
    return {
        "xT": (n((K, S)) * s).astype(np.float32),
        "w": (n((K, N)) / np.sqrt(K) / s).astype(np.float32),
        "b": (0.3 * n((N, 1))).astype(np.float32),
        "gate": np.tile(np.random.uniform(0.2, 1.0, S), (N, 1)).astype(np.float32),
        "offs": striped(np.sort(np.random.permutation(T)[:S])),
    }


def reference(xT, w, b, gate, offs):
    idx = unstriped(offs)
    xq = mxq(f64(xT), 0, "e4m3")
    y = mxq(f64(w), 0, "e4m3").T @ xq
    y = relu(y + f64(b))
    out = np.zeros((N, T))
    out[:, idx] = f64(gate) * y
    return out

@@ -1,0 +1,163 @@
+from contextlib import ExitStack
+
+import concourse.mybir as mybir
+from concourse.masks import make_identity
+
+K, T, S, N = 2048, 1024, 512, 512
+FLOPS = 2 * K * S * N
+
+F32 = mybir.dt.float32
+BF16 = mybir.dt.bfloat16
+U32 = mybir.dt.uint32
+U16 = mybir.dt.uint16
+U8 = mybir.dt.uint8
+FP8X4 = mybir.dt.float8_e4m3fn_x4
+RELU = mybir.ActivationFunctionType.Relu
+
+P = 128
+PACK = 4
+K_PASS = P * PACK
+PASSES = K // K_PASS
+BLOCKS = N // P
+RUN = 4
+
+
+def tile_picked_place_lin_relu_srt_l_kernel(tc, xT, w, b, gate, offs, out):
+    nc = tc.nc
+    with ExitStack() as ctx:
+        keep = ctx.enter_context(tc.tile_pool(name="keep", bufs=1))
+        psum = ctx.enter_context(tc.psum_pool(name="psum", bufs=1))
+
+        offsets = keep.tile([P, S // 16], U16, name="offsets")
+        x_codes = [keep.tile([P, S], U32, name=f"x_codes{c}", align_bytes=64) for c in range(PASSES)]
+        x_scales = [keep.tile([P, S], U8, name=f"x_scales{c}", align_bytes=64) for c in range(PASSES)]
+        w_codes = [keep.tile([P, N], U32, name=f"w_codes{c}", align_bytes=64) for c in range(PASSES)]
+        w_scales = [keep.tile([P, N], U8, name=f"w_scales{c}", align_bytes=64) for c in range(PASSES)]
+        gates = [keep.tile([P, S], F32, name=f"gate{m}") for m in range(2)]
+        gates_late = keep.tile([P, 2, S], F32, name="gates_late")
+        gate_of = [gates[0][:], gates[1][:], gates_late[:, 0, :], gates_late[:, 1, :]]
+        placed = [keep.tile([P, T], F32, name=f"placed{m}") for m in range(BLOCKS)]
+        acts = [keep.tile([P, S], F32, name=f"acts{m}") for m in range(BLOCKS)]
+        sums = [psum.tile([P, S], F32, name=f"sums{m}") for m in range(BLOCKS)]
+
+        def load(name, src, c, lo, hi):
+            raw = keep.tile([P, PACK, hi - lo], F32, name=name)
+            rows = src[c * K_PASS : (c + 1) * K_PASS, lo:hi]
+            nc.sync.dma_start(out=raw[:], in_=rows.rearrange("(p j) n -> p j n", j=PACK))
+            grouped = keep.tile([P, hi - lo, PACK], BF16, name=name + "_bf16", align_bytes=64)
+            return raw, grouped
+
+        def interleave(on_vector, piece, lo, hi):
+            raw, grouped = piece
+            dst = grouped[:, lo:hi, :].rearrange("p (c i) j -> p c j i", i=RUN)
+            src = raw[:, :, lo:hi].rearrange("p j (c i) -> p c j i", i=RUN)
+            if on_vector:
+                nc.vector.tensor_copy(out=dst, in_=src)
+            else:
+                nc.scalar.copy(out=dst, in_=src)
+
+        def quantize(piece, lo, hi, codes, scales, at):
+            cols = slice(at, at + hi - lo)
+            nc.vector.quantize_mx(
+                out=codes[:, cols].bitcast(FP8X4),
+                scales=scales[:, cols],
+                in_=piece[1][:, lo:hi, :].rearrange("p n j -> p (n j)"),
+            )
+
+        def multiply(m, c):
+            cols = slice(m * P, (m + 1) * P)
+            nc.tensor.matmul_mx(
+                out=sums[m][:],
+                lhsT=w_codes[c][:, cols].bitcast(FP8X4),
+                lhsT_scale=w_scales[c][:, cols],
+                rhs=x_codes[c][:].bitcast(FP8X4),
+                rhs_scale=x_scales[c][:],
+                start=(c == 0),
+                stop=(c == PASSES - 1),
+            )
+
+        def activate(m):
+            nc.scalar.activation(out=acts[m][:], in_=sums[m][:], func=RELU, bias=bias[:, m : m + 1])
+
+        def scatter(m):
+            nc.vector.tensor_tensor(
+                placed[m][:].indirect(offsets[:]), acts[m][:], gate_of[m], mybir.AluOpType.mult
+            )
+
+        half = N // 2
+        x0 = load("x0", xT, 0, 0, S)
+        w0 = load("w0", w, 0, 0, N)
+        nc.sync.dma_start(offsets[:], offs)
+        x1 = load("x1", xT, 1, 0, S)
+        w1 = load("w1", w, 1, 0, N)
+        x2 = load("x2", xT, 2, 0, S)
+        x3 = load("x3", xT, 3, 0, S)
+        w2a = load("w2a", w, 2, 0, half)
+        w3a = load("w3a", w, 3, 0, half)
+        w2b = load("w2b", w, 2, half, N)
+        nc.sync.dma_start(out=gates[0][:], in_=gate[0:P, :])
+        w3b = load("w3b", w, 3, half, N)
+        nc.sync.dma_start(out=gates[1][:], in_=gate[P : 2 * P, :])
+        nc.sync.dma_start(out=gates_late[:], in_=gate[2 * P :, :].rearrange("(m p) s -> p m s", p=P))
+
+        bias_rows = keep.tile([P, P], F32, name="bias_rows")
+        identity = keep.tile([P, P], F32, name="identity")
+        bias_turned = psum.tile([P, P], F32, name="bias_turned")
+        bias = keep.tile([P, BLOCKS], F32, name="bias")
+        nc.vector.memset(bias_rows[:], 0.0)
+        nc.scalar.dma_start(out=bias_rows[0:BLOCKS, :], in_=b.rearrange("(m p) o -> m (p o)", p=P))
+        make_identity(nc, identity[:])
+        for m in range(BLOCKS):
+            nc.vector.memset(placed[m][:], 0.0)
+        nc.tensor.transpose(bias_turned[:], bias_rows[:], identity[:])
+        nc.scalar.copy(out=bias[:], in_=bias_turned[:, 0:BLOCKS])
+
+        def whole(piece, codes, scales):
+            interleave(True, piece, 0, half)
+            interleave(False, piece, half, N)
+            quantize(piece, 0, N, codes, scales, 0)
+
+        whole(x0, x_codes[0], x_scales[0])
+        whole(w0, w_codes[0], w_scales[0])
+        for m in range(BLOCKS):
+            multiply(m, 0)
+        whole(x1, x_codes[1], x_scales[1])
+        whole(w1, w_codes[1], w_scales[1])
+        for m in range(BLOCKS):
+            multiply(m, 1)
+        whole(x2, x_codes[2], x_scales[2])
+        whole(x3, x_codes[3], x_scales[3])
+
+        interleave(True, w2a, 0, P)
+        interleave(False, w2a, P, half)
+        quantize(w2a, 0, half, w_codes[2], w_scales[2], 0)
+        multiply(0, 2)
+        multiply(1, 2)
+        interleave(True, w3a, 0, P)
+        interleave(False, w3a, P, half)
+        quantize(w3a, 0, P, w_codes[3], w_scales[3], 0)
+        multiply(0, 3)
+        quantize(w3a, P, half, w_codes[3], w_scales[3], P)
+        multiply(1, 3)
+        interleave(True, w2b, 0, half)
+        activate(0)
+        activate(1)
+        scatter(0)
+        nc.sync.dma_start(out=out[0:P, :], in_=placed[0][:])
+        quantize(w2b, 0, half, w_codes[2], w_scales[2], half)
+        multiply(2, 2)
+        multiply(3, 2)
+        interleave(False, w3b, 0, P)
+        interleave(False, w3b, P, half)
+        quantize(w3b, 0, P, w_codes[3], w_scales[3], half)
+        multiply(2, 3)
+        scatter(1)
+        nc.sync.dma_start(out=out[P : 2 * P, :], in_=placed[1][:])
+        quantize(w3b, P, half, w_codes[3], w_scales[3], half + P)
+        multiply(3, 3)
+        activate(2)
+        activate(3)
+        scatter(2)
+        nc.sync.dma_start(out=out[2 * P : 3 * P, :], in_=placed[2][:])
+        scatter(3)
+        nc.sync.dma_start(out=out[3 * P :, :], in_=placed[3][:])

@@ -33,19 +33,19 @@ def tile_picked_place_lin_relu_srt_l_kernel(tc, xT, w, b, gate, offs, out):
         x_scales = [keep.tile([P, S], U8, name=f"x_scales{c}", align_bytes=64) for c in range(PASSES)]
         w_codes = [keep.tile([P, N], U32, name=f"w_codes{c}", align_bytes=64) for c in range(PASSES)]
         w_scales = [keep.tile([P, N], U8, name=f"w_scales{c}", align_bytes=64) for c in range(PASSES)]
-        gates = [keep.tile([P, S], F32, name=f"gate{m}") for m in range(2)]
-        gates_late = keep.tile([P, 2, S], F32, name="gates_late")
-        gate_of = [gates[0][:], gates[1][:], gates_late[:, 0, :], gates_late[:, 1, :]]
+        gates = [keep.tile([P, S], F32, name=f"gate{m}") for m in range(BLOCKS)]
         placed = [keep.tile([P, T], F32, name=f"placed{m}") for m in range(BLOCKS)]
         acts = [keep.tile([P, S], F32, name=f"acts{m}") for m in range(BLOCKS)]
         sums = [psum.tile([P, S], F32, name=f"sums{m}") for m in range(BLOCKS)]
+
+        def stage(name, width):
+            return keep.tile([P, width, PACK], BF16, name=name + "_bf16", align_bytes=64)
 
         def load(name, src, c, lo, hi):
             raw = keep.tile([P, PACK, hi - lo], F32, name=name)
             rows = src[c * K_PASS : (c + 1) * K_PASS, lo:hi]
             nc.sync.dma_start(out=raw[:], in_=rows.rearrange("(p j) n -> p j n", j=PACK))
-            grouped = keep.tile([P, hi - lo, PACK], BF16, name=name + "_bf16", align_bytes=64)
-            return raw, grouped
+            return raw[:], stage(name, hi - lo)
 
         def interleave(on_vector, piece, lo, hi):
             raw, grouped = piece
@@ -81,24 +81,25 @@ def tile_picked_place_lin_relu_srt_l_kernel(tc, xT, w, b, gate, offs, out):
 
         def scatter(m):
             nc.vector.tensor_tensor(
-                placed[m][:].indirect(offsets[:]), acts[m][:], gate_of[m], mybir.AluOpType.mult
+                placed[m][:].indirect(offsets[:]), acts[m][:], gates[m][:], mybir.AluOpType.mult
             )
 
         half = N // 2
-        x0 = load("x0", xT, 0, 0, S)
-        w0 = load("w0", w, 0, 0, N)
+        x01 = keep.tile([P, 2, PACK, S], F32, name="x01")
+        nc.sync.dma_start(
+            out=x01[:].rearrange("p c j n -> p c (j n)"),
+            in_=xT[0 : 2 * K_PASS, :].rearrange("(c p j) n -> p c (j n)", c=2, j=PACK),
+        )
+        x_pieces = [(x01[:, c, :, :], stage(f"x{c}", S)) for c in range(2)]
         nc.sync.dma_start(offsets[:], offs)
-        x1 = load("x1", xT, 1, 0, S)
-        w1 = load("w1", w, 1, 0, N)
-        x2 = load("x2", xT, 2, 0, S)
-        x3 = load("x3", xT, 3, 0, S)
-        w2a = load("w2a", w, 2, 0, half)
-        w3a = load("w3a", w, 3, 0, half)
-        w2b = load("w2b", w, 2, half, N)
-        nc.sync.dma_start(out=gates[0][:], in_=gate[0:P, :])
-        w3b = load("w3b", w, 3, half, N)
-        nc.sync.dma_start(out=gates[1][:], in_=gate[P : 2 * P, :])
-        nc.sync.dma_start(out=gates_late[:], in_=gate[2 * P :, :].rearrange("(m p) s -> p m s", p=P))
+        x_pieces += [load(f"x{c}", xT, c, 0, S) for c in range(2, PASSES)]
+        w_pieces = {}
+        for m in range(BLOCKS):
+            for c in range(PASSES):
+                w_pieces[m, c] = load(f"w{c}_{m}", w, c, m * P, (m + 1) * P)
+            if m > 0:
+                nc.sync.dma_start(out=gates[m - 1][:], in_=gate[(m - 1) * P : m * P, :])
+        nc.sync.dma_start(out=gates[BLOCKS - 1][:], in_=gate[N - P :, :])
 
         bias_rows = keep.tile([P, P], F32, name="bias_rows")
         identity = keep.tile([P, P], F32, name="identity")
@@ -115,49 +116,23 @@ def tile_picked_place_lin_relu_srt_l_kernel(tc, xT, w, b, gate, offs, out):
         def whole(piece, codes, scales):
             interleave(True, piece, 0, half)
             interleave(False, piece, half, N)
-            quantize(piece, 0, N, codes, scales, 0)
+            quantize(piece, 0, half, codes, scales, 0)
+            quantize(piece, half, N, codes, scales, half)
 
-        whole(x0, x_codes[0], x_scales[0])
-        whole(w0, w_codes[0], w_scales[0])
-        for m in range(BLOCKS):
-            multiply(m, 0)
-        whole(x1, x_codes[1], x_scales[1])
-        whole(w1, w_codes[1], w_scales[1])
-        for m in range(BLOCKS):
-            multiply(m, 1)
-        whole(x2, x_codes[2], x_scales[2])
-        whole(x3, x_codes[3], x_scales[3])
+        def put_back(m):
+            scatter(m)
+            nc.sync.dma_start(out=out[m * P : (m + 1) * P, :], in_=placed[m][:])
 
-        interleave(True, w2a, 0, P)
-        interleave(False, w2a, P, half)
-        quantize(w2a, 0, half, w_codes[2], w_scales[2], 0)
-        multiply(0, 2)
-        multiply(1, 2)
-        interleave(True, w3a, 0, P)
-        interleave(False, w3a, P, half)
-        quantize(w3a, 0, P, w_codes[3], w_scales[3], 0)
-        multiply(0, 3)
-        quantize(w3a, P, half, w_codes[3], w_scales[3], P)
-        multiply(1, 3)
-        interleave(True, w2b, 0, half)
-        activate(0)
-        activate(1)
-        scatter(0)
-        nc.sync.dma_start(out=out[0:P, :], in_=placed[0][:])
-        quantize(w2b, 0, half, w_codes[2], w_scales[2], half)
-        multiply(2, 2)
-        multiply(3, 2)
-        interleave(False, w3b, 0, P)
-        interleave(False, w3b, P, half)
-        quantize(w3b, 0, P, w_codes[3], w_scales[3], half)
-        multiply(2, 3)
-        scatter(1)
-        nc.sync.dma_start(out=out[P : 2 * P, :], in_=placed[1][:])
-        quantize(w3b, P, half, w_codes[3], w_scales[3], half + P)
-        multiply(3, 3)
-        activate(2)
-        activate(3)
-        scatter(2)
-        nc.sync.dma_start(out=out[2 * P : 3 * P, :], in_=placed[2][:])
-        scatter(3)
-        nc.sync.dma_start(out=out[3 * P :, :], in_=placed[3][:])
+        for c in range(PASSES):
+            whole(x_pieces[c], x_codes[c], x_scales[c])
+        for m in range(BLOCKS):
+            first_on_vector = 2 if m < 2 else 3
+            for c in range(PASSES):
+                interleave(c >= first_on_vector, w_pieces[m, c], 0, P)
+                quantize(w_pieces[m, c], 0, P, w_codes[c], w_scales[c], m * P)
+                multiply(m, c)
+            if m > 0:
+                activate(m - 1)
+                put_back(m - 1)
+        activate(BLOCKS - 1)
+        put_back(BLOCKS - 1)

@@ -85,21 +85,26 @@ def tile_picked_place_lin_relu_srt_l_kernel(tc, xT, w, b, gate, offs, out):
             )
 
         half = N // 2
-        x01 = keep.tile([P, 2, PACK, S], F32, name="x01")
-        nc.sync.dma_start(
-            out=x01[:].rearrange("p c j n -> p c (j n)"),
-            in_=xT[0 : 2 * K_PASS, :].rearrange("(c p j) n -> p c (j n)", c=2, j=PACK),
-        )
-        x_pieces = [(x01[:, c, :, :], stage(f"x{c}", S)) for c in range(2)]
+        x_pieces = [load(f"x{c}", xT, c, 0, S) for c in range(2)]
         nc.sync.dma_start(offsets[:], offs)
         x_pieces += [load(f"x{c}", xT, c, 0, S) for c in range(2, PASSES)]
+        last = PASSES - 1
         w_pieces = {}
+
+        def load_gate(m):
+            nc.sync.dma_start(out=gates[m][:], in_=gate[m * P : (m + 1) * P, :])
+
+        for c in range(last):
+            piece = load(f"w{c}_01", w, c, 0, half)
+            w_pieces[0, c] = (piece, 0)
+            w_pieces[1, c] = (piece, P)
         for m in range(BLOCKS):
             for c in range(PASSES):
-                w_pieces[m, c] = load(f"w{c}_{m}", w, c, m * P, (m + 1) * P)
+                if (m, c) not in w_pieces:
+                    w_pieces[m, c] = (load(f"w{c}_{m}", w, c, m * P, (m + 1) * P), 0)
             if m > 0:
-                nc.sync.dma_start(out=gates[m - 1][:], in_=gate[(m - 1) * P : m * P, :])
-        nc.sync.dma_start(out=gates[BLOCKS - 1][:], in_=gate[N - P :, :])
+                load_gate(m - 1)
+        load_gate(BLOCKS - 1)
 
         bias_rows = keep.tile([P, P], F32, name="bias_rows")
         identity = keep.tile([P, P], F32, name="identity")
@@ -125,14 +130,22 @@ def tile_picked_place_lin_relu_srt_l_kernel(tc, xT, w, b, gate, offs, out):
 
         for c in range(PASSES):
             whole(x_pieces[c], x_codes[c], x_scales[c])
-        for m in range(BLOCKS):
-            first_on_vector = 2 if m < 2 else 3
+
+        def step(on_vector, m, c):
+            piece, lo = w_pieces[m, c]
+            interleave(on_vector, piece, lo, lo + P)
+            quantize(piece, lo, lo + P, w_codes[c], w_scales[c], m * P)
+            multiply(m, c)
+
+        for c in range(PASSES):
+            step(True, 0, c)
+            step(False, 1, c)
+        activate(0)
+        put_back(0)
+        for m in range(2, BLOCKS):
             for c in range(PASSES):
-                interleave(c >= first_on_vector, w_pieces[m, c], 0, P)
-                quantize(w_pieces[m, c], 0, P, w_codes[c], w_scales[c], m * P)
-                multiply(m, c)
-            if m > 0:
-                activate(m - 1)
-                put_back(m - 1)
+                step(c == last, m, c)
+            activate(m - 1)
+            put_back(m - 1)
         activate(BLOCKS - 1)
         put_back(BLOCKS - 1)

from contextlib import ExitStack

import concourse.mybir as mybir
from concourse.masks import make_identity

K, T, S, N = 2048, 1024, 512, 512
FLOPS = 2 * K * S * N

F32 = mybir.dt.float32
BF16 = mybir.dt.bfloat16
U32 = mybir.dt.uint32
U16 = mybir.dt.uint16
U8 = mybir.dt.uint8
FP8X4 = mybir.dt.float8_e4m3fn_x4
RELU = mybir.ActivationFunctionType.Relu

P = 128
PACK = 4
K_PASS = P * PACK
PASSES = K // K_PASS
BLOCKS = N // P
RUN = 4


def tile_picked_place_lin_relu_srt_l_kernel(tc, xT, w, b, gate, offs, out):
    nc = tc.nc
    with ExitStack() as ctx:
        keep = ctx.enter_context(tc.tile_pool(name="keep", bufs=1))
        psum = ctx.enter_context(tc.psum_pool(name="psum", bufs=1))

        offsets = keep.tile([P, S // 16], U16, name="offsets")
        x_codes = [keep.tile([P, S], U32, name=f"x_codes{c}", align_bytes=64) for c in range(PASSES)]
        x_scales = [keep.tile([P, S], U8, name=f"x_scales{c}", align_bytes=64) for c in range(PASSES)]
        w_codes = [keep.tile([P, N], U32, name=f"w_codes{c}", align_bytes=64) for c in range(PASSES)]
        w_scales = [keep.tile([P, N], U8, name=f"w_scales{c}", align_bytes=64) for c in range(PASSES)]
        gates = [keep.tile([P, S], F32, name=f"gate{m}") for m in range(BLOCKS)]
        placed = [keep.tile([P, T], F32, name=f"placed{m}") for m in range(BLOCKS)]
        acts = [keep.tile([P, S], F32, name=f"acts{m}") for m in range(BLOCKS)]
        sums = [psum.tile([P, S], F32, name=f"sums{m}") for m in range(BLOCKS)]

        def stage(name, width):
            return keep.tile([P, width, PACK], BF16, name=name + "_bf16", align_bytes=64)

        def load(name, src, c, lo, hi):
            raw = keep.tile([P, PACK, hi - lo], F32, name=name)
            rows = src[c * K_PASS : (c + 1) * K_PASS, lo:hi]
            nc.sync.dma_start(out=raw[:], in_=rows.rearrange("(p j) n -> p j n", j=PACK))
            return raw[:], stage(name, hi - lo)

        def interleave(on_vector, piece, lo, hi):
            raw, grouped = piece
            dst = grouped[:, lo:hi, :].rearrange("p (c i) j -> p c j i", i=RUN)
            src = raw[:, :, lo:hi].rearrange("p j (c i) -> p c j i", i=RUN)
            if on_vector:
                nc.vector.tensor_copy(out=dst, in_=src)
            else:
                nc.scalar.copy(out=dst, in_=src)

        def quantize(piece, lo, hi, codes, scales, at):
            cols = slice(at, at + hi - lo)
            nc.vector.quantize_mx(
                out=codes[:, cols].bitcast(FP8X4),
                scales=scales[:, cols],
                in_=piece[1][:, lo:hi, :].rearrange("p n j -> p (n j)"),
            )

        def multiply(m, c):
            cols = slice(m * P, (m + 1) * P)
            nc.tensor.matmul_mx(
                out=sums[m][:],
                lhsT=w_codes[c][:, cols].bitcast(FP8X4),
                lhsT_scale=w_scales[c][:, cols],
                rhs=x_codes[c][:].bitcast(FP8X4),
                rhs_scale=x_scales[c][:],
                start=(c == 0),
                stop=(c == PASSES - 1),
            )

        def activate(m):
            nc.scalar.activation(out=acts[m][:], in_=sums[m][:], func=RELU, bias=bias[:, m : m + 1])

        def scatter(m):
            nc.vector.tensor_tensor(
                placed[m][:].indirect(offsets[:]), acts[m][:], gates[m][:], mybir.AluOpType.mult
            )

        half = N // 2
        x_pieces = [load(f"x{c}", xT, c, 0, S) for c in range(2)]
        nc.sync.dma_start(offsets[:], offs)
        x_pieces += [load(f"x{c}", xT, c, 0, S) for c in range(2, PASSES)]
        last = PASSES - 1
        w_pieces = {}

        def load_gate(m):
            nc.sync.dma_start(out=gates[m][:], in_=gate[m * P : (m + 1) * P, :])

        for c in range(last):
            piece = load(f"w{c}_01", w, c, 0, half)
            w_pieces[0, c] = (piece, 0)
            w_pieces[1, c] = (piece, P)
        for m in range(BLOCKS):
            for c in range(PASSES):
                if (m, c) not in w_pieces:
                    w_pieces[m, c] = (load(f"w{c}_{m}", w, c, m * P, (m + 1) * P), 0)
            if m > 0:
                load_gate(m - 1)
        load_gate(BLOCKS - 1)

        bias_rows = keep.tile([P, P], F32, name="bias_rows")
        identity = keep.tile([P, P], F32, name="identity")
        bias_turned = psum.tile([P, P], F32, name="bias_turned")
        bias = keep.tile([P, BLOCKS], F32, name="bias")
        nc.vector.memset(bias_rows[:], 0.0)
        nc.scalar.dma_start(out=bias_rows[0:BLOCKS, :], in_=b.rearrange("(m p) o -> m (p o)", p=P))
        make_identity(nc, identity[:])
        for m in range(BLOCKS):
            nc.vector.memset(placed[m][:], 0.0)
        nc.tensor.transpose(bias_turned[:], bias_rows[:], identity[:])
        nc.scalar.copy(out=bias[:], in_=bias_turned[:, 0:BLOCKS])

        def whole(piece, codes, scales):
            interleave(True, piece, 0, half)
            interleave(False, piece, half, N)
            quantize(piece, 0, half, codes, scales, 0)
            quantize(piece, half, N, codes, scales, half)

        def put_back(m):
            scatter(m)
            nc.sync.dma_start(out=out[m * P : (m + 1) * P, :], in_=placed[m][:])

        for c in range(PASSES):
            whole(x_pieces[c], x_codes[c], x_scales[c])

        def step(on_vector, m, c):
            piece, lo = w_pieces[m, c]
            interleave(on_vector, piece, lo, lo + P)
            quantize(piece, lo, lo + P, w_codes[c], w_scales[c], m * P)
            multiply(m, c)

        for c in range(PASSES):
            step(True, 0, c)
            step(False, 1, c)
        activate(0)
        put_back(0)
        for m in range(2, BLOCKS):
            for c in range(PASSES):
                step(c == last, m, c)
            activate(m - 1)
            put_back(m - 1)
        activate(BLOCKS - 1)
        put_back(BLOCKS - 1)
